import numpy as np
import ml_dtypes


def mxq(x, axis, fmt="e4m3"):
    dtype, down = {"e4m3": (ml_dtypes.float8_e4m3fn, 7), "e5m2": (ml_dtypes.float8_e5m2, 14)}[fmt]
    v = np.moveaxis(np.asarray(x, np.float32).astype(ml_dtypes.bfloat16).astype(np.float64), axis, -1)
    blocks = v.reshape(v.shape[:-1] + (-1, 32))
    amax = np.abs(blocks).max(-1, keepdims=True)
    byte = np.maximum(np.where(amax > 0, np.frexp(amax)[1] - 1 + 127, 0) - down, 1)
    scale = np.exp2(byte - 127.0)
    codes = (blocks / scale).astype(np.float32).astype(dtype).astype(np.float64)
    return np.moveaxis((codes * scale).reshape(v.shape), -1, axis)


WIDE = False


def mx_kscale(k):
    if not WIDE:
        return np.ones(k)
    levels = np.array([30, -30])
    if k % 512:
        return np.exp2(np.random.permutation(np.resize(levels, k // 32))).repeat(32)
    a = np.empty((k // 512, 16))
    for p in range(k // 512):
        a[p, :8] = np.random.permutation(np.resize(levels, 8))
        for g in range(8):
            far = levels[np.abs(levels - a[p, g]) >= 10]
            a[p, g + 8] = far[np.random.randint(len(far))]
    return np.exp2(a.ravel()).repeat(32)


def f64(x):
    return np.asarray(x).astype(np.float64)


def striped(idx):
    return np.tile(np.asarray(idx).reshape(-1, 16).T, (8, 1)).astype(np.uint16)


def unstriped(offs):
    return offs[:16].T.reshape(-1).astype(np.int64)


E2M1 = np.array([0.0, 0.5, 1.0, 1.5, 2.0, 3.0, 4.0, 6.0, -0.0, -0.5, -1.0, -1.5, -2.0, -3.0, -4.0, -6.0])


def pack_weight(w, fmt):
    k, n = w.shape
    w = f64(np.asarray(w, np.float32).astype(ml_dtypes.bfloat16)).reshape(k // 32, 32, n)
    amax = np.abs(w).max(1)
    if fmt in ("e4m3", "e5m2"):
        byte = np.frexp(amax)[1] - 1 + 127 - (7 if fmt == "e4m3" else 14)
    else:
        mant, ex = np.frexp(amax / 6.0)
        byte = np.where(mant > 0.5, ex, ex - 1) + 127
    byte = np.clip(np.where(amax > 0, byte, 1), 1, 254)
    scaled = (w * np.exp2(127.0 - byte)[:, None, :]).reshape(k, n).astype(np.float32)
    by_word = np.ascontiguousarray(scaled.reshape(k // 512, 128, 4, n).transpose(0, 1, 3, 2))
    if fmt in ("e4m3", "e5m2"):
        words = by_word.astype(ml_dtypes.float8_e4m3fn if fmt == "e4m3" else ml_dtypes.float8_e5m2).view(np.uint8)
    else:
        c = by_word.astype(ml_dtypes.float4_e2m1fn).view(np.uint8) & 0xF
        words = (c[..., 0::2] | (c[..., 1::2] << 4)).reshape(k // 512, 128, 2 * n)
    return np.ascontiguousarray(words), np.ascontiguousarray(byte.astype(np.uint8).reshape(k // 512, 16, n))


def unpack_weight(words, scales, fmt):
    g, _, n = scales.shape
    words = np.ascontiguousarray(words).reshape(g, 128, n, -1)
    if fmt in ("e4m3", "e5m2"):
        vals = words.view(ml_dtypes.float8_e4m3fn if fmt == "e4m3" else ml_dtypes.float8_e5m2).astype(np.float64)
    else:
        nib = np.empty((g, 128, n, 4), np.uint8)
        nib[..., 0::2] = words & 0xF
        nib[..., 1::2] = words >> 4
        vals = E2M1[nib]
    vals = vals * np.repeat(np.exp2(scales.astype(np.float64) - 127.0), 8, axis=1)[..., None]
    return vals.transpose(0, 1, 3, 2).reshape(g * 512, n)


def sigmoid(v):
    return 1.0 / (1.0 + np.exp(-v))


def sgn(shape):
    return np.random.uniform(0.5, 2.0, shape) * np.where(np.random.standard_normal(shape) < 0, -1.0, 1.0)


K, T, J, R, F, Z, O, N, E = 512, 1024, 256, 512, 512, 1024, 128, 256, 512


def setup_inputs():
    n = np.random.standard_normal
    idx = np.random.permutation(T)[:J]
    idx2 = np.random.permutation(Z)[:J]
    idx3 = np.random.permutation(J)[:O]
    idx4 = np.random.permutation(J)[:O]
    idx5 = np.random.permutation(E)[:O]
    idx6 = np.random.permutation(E)[:O]
    fk = mx_kscale(K)
    ff = mx_kscale(F)
    fr = mx_kscale(R)
    xtp = pack_weight(n((K, T)) / fk[:, None], "e2m1")
    xop = pack_weight(n((F, Z)) / ff[:, None], "e5m2")
    wp = pack_weight(n((K, R)) * 1 / np.sqrt(K) * fk[:, None], "e5m2")
    w0p = pack_weight(n((F, R)) * 1 / np.sqrt(F) * ff[:, None], "e4m3")
    wbp = pack_weight(n((R, N)) * 1 / np.sqrt(R) / fr[:, None], "e4m3")
    return {
        "xt_words": xtp[0],
        "xt_scales": xtp[1],
        "xo_words": xop[0],
        "xo_scales": xop[1],
        "w_words": wp[0],
        "w_scales": wp[1],
        "w0_words": w0p[0],
        "w0_scales": w0p[1],
        "sa": (np.random.uniform(0.5, 1.6, (R, 1)) * fr[:, None]).astype(np.float32),
        "sg": (sgn((R, 1))).astype(np.float32),
        "bg": (np.random.uniform(-2.0, 2.0, (R, 1))).astype(np.float32),
        "wb_words": wbp[0],
        "wb_scales": wbp[1],
        "offs": striped(idx),
        "offs2": striped(idx2),
        "offs3": striped(idx3),
        "offs4": striped(idx4),
        "offs5": striped(idx5),
        "offs6": striped(idx6),
    }


def reference(xt_words, xt_scales, xo_words, xo_scales, w_words, w_scales, w0_words, w0_scales, sa, sg, bg, wb_words, wb_scales, offs, offs2, offs3, offs4, offs5, offs6):
    idx = unstriped(offs)
    idx2 = unstriped(offs2)
    idx3 = unstriped(offs3)
    idx4 = unstriped(offs4)
    idx5 = unstriped(offs5)
    idx6 = unstriped(offs6)
    xtu = unpack_weight(xt_words, xt_scales, "e2m1")
    xou = unpack_weight(xo_words, xo_scales, "e5m2")
    wu = unpack_weight(w_words, w_scales, "e5m2")
    w0u = unpack_weight(w0_words, w0_scales, "e4m3")
    wbu = unpack_weight(wb_words, wb_scales, "e4m3")
    xtidxg = xtu[:, idx]
    xoidx2g = xou[:, idx2]
    a = wu.T @ xtidxg + w0u.T @ xoidx2g
    hid = a[:, idx3] * f64(sa) * sigmoid(a[:, idx4] * f64(sg) + f64(bg))
    hidq = mxq(hid, 0, "e5m2")
    p = wbu.T @ hidq
    pa = np.zeros((N, E))
    pa[:, idx5] = p
    pb = np.zeros((N, E))
    pb[:, idx6] = p
    y = pa + pb
    return y

@@ -1,0 +1,171 @@
+from contextlib import ExitStack
+
+import concourse.mybir as mybir
+
+K, T, J, R, F, Z, O, N, E = 512, 1024, 256, 512, 512, 1024, 128, 256, 512
+FLOPS = 2 * K * R * J + 2 * F * R * J + 2 * R * N * O
+
+F32 = mybir.dt.float32
+BF16 = mybir.dt.bfloat16
+I32 = mybir.dt.int32
+U32 = mybir.dt.uint32
+U16 = mybir.dt.uint16
+U8 = mybir.dt.uint8
+E4M3 = mybir.dt.float8_e4m3fn_x4
+E5M2 = mybir.dt.float8_e5m2_x4
+E2M1 = mybir.dt.float4_e2m1fn_x4
+ACT = mybir.ActivationFunctionType
+ALU = mybir.AluOpType
+
+P = 128
+HALF = 64
+PACK = 4
+
+
+def tile_list_gatedpick_bank_one_pagetwice_kernel(
+    tc, xt_words, xt_scales, xo_words, xo_scales, w_words, w_scales, w0_words, w0_scales,
+    sa, sg, bg, wb_words, wb_scales, offs, offs2, offs3, offs4, offs5, offs6, out,
+):
+    nc = tc.nc
+
+    def words_of(packed):
+        return packed[0].rearrange("p c b -> p (c b)").bitcast(I32)
+
+    def load_scale_rows(scales, stage, base):
+        rows = scales[0].bitcast(I32).rearrange("(h q r) c -> q r h c", h=2, q=2)
+        for q in range(2):
+            first = base + 32 * q
+            nc.sync.dma_start(out=stage[first : first + 4], in_=rows[q])
+
+    with ExitStack() as ctx:
+        lists = ctx.enter_context(tc.tile_pool(name="lists", bufs=1))
+        sb = ctx.enter_context(tc.tile_pool(name="sb", bufs=1))
+        psum = ctx.enter_context(tc.psum_pool(name="psum", bufs=1))
+
+        l1 = lists.tile([P, J // 16], U16, name="l1")
+        l2 = lists.tile([P, J // 16], U16, name="l2")
+        l3 = lists.tile([P, O // 16], U16, name="l3")
+        l4 = lists.tile([P, O // 16], U16, name="l4")
+        l5 = lists.tile([P, O // 16], U16, name="l5")
+        l6 = lists.tile([P, O // 16], U16, name="l6")
+
+        xt_stage = sb.tile([P, 2, T // 4], I32, name="xt_stage")
+        xo_stage = sb.tile([P, 2, Z // 4], I32, name="xo_stage")
+        ws = sb.tile([P, 3, R], U8, name="ws")
+        wb_plane = sb.tile([P, N], U8, name="wb_plane", align_bytes=64)
+        ws32 = ws[:].bitcast(I32)
+        nc.vector.memset(xt_stage[0:HALF], 0)
+        nc.vector.memset(xo_stage[HALF:P], 0)
+        nc.vector.memset(ws32, 0)
+        nc.vector.memset(wb_plane[:].bitcast(I32), 0)
+
+        xt_tab = sb.tile([P, T], U16, name="xt_tab")
+        xo_tab = sb.tile([P, Z], U32, name="xo_tab")
+        w_raw = sb.tile([P, R], U32, name="w_raw")
+        w0_raw = sb.tile([P, R], U32, name="w0_raw")
+        wb_codes = sb.tile([P, N], U32, name="wb_codes", align_bytes=64)
+        sa_t = sb.tile([P, PACK], F32, name="sa_t")
+        sg_t = sb.tile([P, PACK], F32, name="sg_t")
+        bg_t = sb.tile([P, PACK], F32, name="bg_t")
+
+        nc.scalar.dma_start(out=xt_tab[:].bitcast(I32), in_=xt_words[0].bitcast(I32))
+        nc.scalar.dma_start(out=xo_tab[:].bitcast(I32), in_=words_of(xo_words))
+        nc.sync.dma_start(l1[:], offs)
+        load_scale_rows(xt_scales, xt_stage, 0)
+        nc.sync.dma_start(l2[:], offs2)
+        load_scale_rows(xo_scales, xo_stage, HALF)
+        load_scale_rows(w_scales, ws32[:, 0:2, :], 0)
+        load_scale_rows(w0_scales, ws32[:, 1:3, :], HALF)
+        nc.sync.dma_start(out=w_raw[:].bitcast(I32), in_=words_of(w_words))
+        nc.sync.dma_start(out=w0_raw[:].bitcast(I32), in_=words_of(w0_words))
+        for tile, vec in ((sg_t, sg), (bg_t, bg), (sa_t, sa)):
+            nc.gpsimd.dma_start(out=tile[:], in_=vec.rearrange("(p t) o -> p (t o)", t=PACK))
+        nc.sync.dma_start(l4[:], offs4)
+        nc.sync.dma_start(l3[:], offs3)
+        nc.sync.dma_start(out=wb_codes[:].bitcast(I32), in_=words_of(wb_words))
+        wb_rows = wb_scales[0].bitcast(I32)
+        for quad in range(4):
+            nc.sync.dma_start(out=wb_plane[:].bitcast(I32)[32 * quad : 32 * quad + 4], in_=wb_rows[4 * quad : 4 * quad + 4])
+        nc.sync.dma_start(l5[:], offs5)
+        nc.sync.dma_start(l6[:], offs6)
+
+        xt_plane = sb.tile([P, T], U8, name="xt_plane")
+        xo_plane = sb.tile([P, Z], U8, name="xo_plane")
+        xt_codes = sb.tile([P, J], U16, name="xt_codes", align_bytes=64)
+        xt_sc = sb.tile([P, J], U8, name="xt_sc", align_bytes=64)
+        xo_codes = sb.tile([P, J], U32, name="xo_codes", align_bytes=64)
+        xo_sc = sb.tile([P, J], U8, name="xo_sc", align_bytes=64)
+
+        def spread(plane, stage, base):
+            for h in range(2):
+                nc.vector.tensor_copy(out=plane[:].bitcast(I32)[HALF * h : HALF * (h + 1)], in_=stage[base : base + HALF, h, :])
+
+        w_codes = sb.tile([P, PACK, P], U32, name="w_codes", align_bytes=64)
+        w0_codes = sb.tile([P, PACK, P], U32, name="w0_codes", align_bytes=64)
+        for codes, raw in ((w_codes, w_raw), (w0_codes, w0_raw)):
+            nc.scalar.copy(out=codes[:].rearrange("p t m -> p m t"), in_=raw[:].rearrange("p (m t) -> p m t", t=PACK))
+
+        wsc = [sb.tile([P, 2, P], U8, name="wsc%d" % t, tag="late%d" % t, align_bytes=64) for t in range(PACK)]
+
+        def deal_scales(t):
+            nc.vector.tensor_copy(out=wsc[t][:], in_=ws[:, 0:3:2, :].rearrange("p s (m t) -> p s m t", t=PACK)[:, :, :, t])
+
+        spread(xt_plane, xt_stage, 0)
+        nc.vector.tensor_copy(xt_codes[:], xt_tab[:].indirect(l1[:]))
+        nc.vector.tensor_copy(xt_sc[:], xt_plane[:].indirect(l1[:]))
+        spread(xo_plane, xo_stage, HALF)
+        nc.vector.tensor_copy(xo_codes[:], xo_tab[:].indirect(l2[:]))
+        nc.vector.tensor_copy(out=ws32[HALF:P, 0, :], in_=ws32[0:HALF, 1, :])
+        nc.vector.tensor_copy(out=ws32[0:HALF, 2, :], in_=ws32[HALF:P, 1, :])
+        deal_scales(0)
+        nc.vector.tensor_copy(xo_sc[:], xo_plane[:].indirect(l2[:]))
+
+        picked = sb.tile([P, PACK, O], F32, name="picked")
+        gate = sb.tile([P, PACK, O], F32, name="gate")
+        hid = sb.tile([P, O, PACK], BF16, name="hid", align_bytes=64)
+        for t in range(PACK):
+            if t > 0:
+                deal_scales(t)
+            acc = psum.tile([P, J], F32, name="acc%d" % t)
+            nc.tensor.matmul_mx(out=acc[:], lhsT=w_codes[:, t, :].bitcast(E5M2), lhsT_scale=wsc[t][:, 0, :],
+                                rhs=xt_codes[:].bitcast(E2M1), rhs_scale=xt_sc[:], start=True, stop=False)
+            nc.tensor.matmul_mx(out=acc[:], lhsT=w0_codes[:, t, :].bitcast(E4M3), lhsT_scale=wsc[t][:, 1, :],
+                                rhs=xo_codes[:].bitcast(E5M2), rhs_scale=xo_sc[:], start=False, stop=True)
+            a_rows = sb.tile([P, J], F32, name="a%d" % t)
+            nc.vector.tensor_copy(out=a_rows[:], in_=acc[:])
+            nc.scalar.activation(out=gate[:, t, :], in_=a_rows[:].indirect(l4[:]), func=ACT.Sigmoid,
+                                 bias=bg_t[:, t : t + 1], scale=sg_t[:, t : t + 1])
+            nc.scalar.activation(out=picked[:, t, :], in_=a_rows[:].indirect(l3[:]), func=ACT.Copy,
+                                 scale=sa_t[:, t : t + 1])
+            if t % 2 == 1:
+                pair = slice(t - 1, t + 1)
+                nc.vector.tensor_tensor(out=hid[:, :, pair], in0=picked[:, pair, :].rearrange("p t o -> p o t"),
+                                        in1=gate[:, pair, :].rearrange("p t o -> p o t"), op=ALU.mult)
+
+        hid_codes = sb.tile([P, O], U32, name="hid_codes", align_bytes=64)
+        hid_sc = sb.tile([P, O], U8, name="hid_sc", align_bytes=64)
+        nc.vector.quantize_mx(out=hid_codes[:].bitcast(E5M2), scales=hid_sc[:], in_=hid[:].rearrange("p o t -> p (o t)"))
+
+        pages = [sb.tile([P, E], F32, name="page%d" % i, tag="late%d" % i, align_bytes=64) for i in range(4)]
+        for page in pages:
+            nc.gpsimd.memset(page[:], 0.0)
+
+        prod = []
+        for h in range(2):
+            cols = slice(P * h, P * (h + 1))
+            acc2 = psum.tile([P, O], F32, name="acc2_%d" % h)
+            nc.tensor.matmul_mx(out=acc2[:], lhsT=wb_codes[:, cols].bitcast(E4M3), lhsT_scale=wb_plane[:, cols],
+                                rhs=hid_codes[:].bitcast(E5M2), rhs_scale=hid_sc[:], start=True, stop=True)
+            rows = sb.tile([P, O], F32, name="prod%d" % h)
+            if h == 0:
+                nc.vector.tensor_copy(out=rows[:], in_=acc2[:])
+            else:
+                nc.scalar.copy(out=rows[:], in_=acc2[:])
+            prod.append(rows)
+        for h in range(2):
+            page_a, page_b = pages[2 * h], pages[2 * h + 1]
+            nc.vector.tensor_copy(page_a[:].indirect(l5[:]), prod[h][:])
+            nc.scalar.activation(out=page_b[:].indirect(l6[:]), in_=prod[h][:], func=ACT.Copy)
+            total = sb.tile([P, E], F32, name="total%d" % h)
+            nc.vector.tensor_tensor(out=total[:], in0=page_a[:], in1=page_b[:], op=ALU.add)
+            nc.sync.dma_start(out=out[P * h : P * (h + 1), :], in_=total[:])

@@ -31,11 +31,12 @@ def tile_list_gatedpick_bank_one_pagetwice_kernel(
     def words_of(packed):
         return packed[0].rearrange("p c b -> p (c b)").bitcast(I32)
 
-    def load_scale_rows(scales, stage, base):
-        rows = scales[0].bitcast(I32).rearrange("(h q r) c -> q r h c", h=2, q=2)
-        for q in range(2):
-            first = base + 32 * q
-            nc.sync.dma_start(out=stage[first : first + 4], in_=rows[q])
+    def load_quadrant(engine, scales, plane, quad):
+        rows = scales[0].bitcast(I32)
+        engine.dma_start(out=plane[:].bitcast(I32)[32 * quad : 32 * quad + 4], in_=rows[4 * quad : 4 * quad + 4])
+
+    def load_column(tile, vec):
+        nc.sync.dma_start(out=tile[:], in_=vec.rearrange("(p t) o -> p (t o)", t=PACK))
 
     with ExitStack() as ctx:
         lists = ctx.enter_context(tc.tile_pool(name="lists", bufs=1))
@@ -49,15 +50,20 @@ def tile_list_gatedpick_bank_one_pagetwice_kernel(
         l5 = lists.tile([P, O // 16], U16, name="l5")
         l6 = lists.tile([P, O // 16], U16, name="l6")
 
-        xt_stage = sb.tile([P, 2, T // 4], I32, name="xt_stage")
-        xo_stage = sb.tile([P, 2, Z // 4], I32, name="xo_stage")
-        ws = sb.tile([P, 3, R], U8, name="ws")
+        xt_plane = sb.tile([P, T], U8, name="xt_plane")
+        xo_plane = sb.tile([P, Z], U8, name="xo_plane")
+        ws_stage = sb.tile([4, 4, 2, R // 4], I32, name="ws_stage")
+        ws = sb.tile([P, 2, R], U8, name="ws")
         wb_plane = sb.tile([P, N], U8, name="wb_plane", align_bytes=64)
         ws32 = ws[:].bitcast(I32)
-        nc.vector.memset(xt_stage[0:HALF], 0)
-        nc.vector.memset(xo_stage[HALF:P], 0)
+        nc.vector.memset(xt_plane[:].bitcast(I32), 0)
+        nc.vector.memset(xo_plane[:].bitcast(I32), 0)
         nc.vector.memset(ws32, 0)
-        nc.vector.memset(wb_plane[:].bitcast(I32), 0)
+
+        warm_in = sb.tile([P, 1], F32, name="warm_in")
+        warm_out = sb.tile([P, 1], F32, name="warm_out")
+        nc.vector.memset(warm_in[:], 0.0)
+        nc.scalar.activation(out=warm_out[:], in_=warm_in[:], func=ACT.Sigmoid)
 
         xt_tab = sb.tile([P, T], U16, name="xt_tab")
         xo_tab = sb.tile([P, Z], U32, name="xo_tab")
@@ -68,37 +74,37 @@ def tile_list_gatedpick_bank_one_pagetwice_kernel(
         sg_t = sb.tile([P, PACK], F32, name="sg_t")
         bg_t = sb.tile([P, PACK], F32, name="bg_t")
 
-        nc.scalar.dma_start(out=xt_tab[:].bitcast(I32), in_=xt_words[0].bitcast(I32))
-        nc.scalar.dma_start(out=xo_tab[:].bitcast(I32), in_=words_of(xo_words))
+        for s, scales in enumerate((w_scales, w0_scales)):
+            nc.sync.dma_start(out=ws_stage[:, :, s, :], in_=scales[0].bitcast(I32).rearrange("(q r) c -> r q c", r=4))
         nc.sync.dma_start(l1[:], offs)
-        load_scale_rows(xt_scales, xt_stage, 0)
         nc.sync.dma_start(l2[:], offs2)
-        load_scale_rows(xo_scales, xo_stage, HALF)
-        load_scale_rows(w_scales, ws32[:, 0:2, :], 0)
-        load_scale_rows(w0_scales, ws32[:, 1:3, :], HALF)
+        for quad in (0, 1):
+            load_quadrant(nc.sync, xt_scales, xt_plane, quad)
+        nc.sync.dma_start(out=xt_tab[:].bitcast(I32), in_=xt_words[0].bitcast(I32))
+        nc.sync.dma_start(out=xo_tab[:].bitcast(I32), in_=words_of(xo_words))
+        for quad in (2, 3):
+            load_quadrant(nc.sync, xt_scales, xt_plane, quad)
+        for quad in (0, 1):
+            load_quadrant(nc.sync, xo_scales, xo_plane, quad)
+        for quad in (2, 3):
+            load_quadrant(nc.gpsimd, xo_scales, xo_plane, quad)
         nc.sync.dma_start(out=w_raw[:].bitcast(I32), in_=words_of(w_words))
         nc.sync.dma_start(out=w0_raw[:].bitcast(I32), in_=words_of(w0_words))
-        for tile, vec in ((sg_t, sg), (bg_t, bg), (sa_t, sa)):
-            nc.gpsimd.dma_start(out=tile[:], in_=vec.rearrange("(p t) o -> p (t o)", t=PACK))
         nc.sync.dma_start(l4[:], offs4)
+        load_column(sg_t, sg)
+        load_column(bg_t, bg)
         nc.sync.dma_start(l3[:], offs3)
+        load_column(sa_t, sa)
         nc.sync.dma_start(out=wb_codes[:].bitcast(I32), in_=words_of(wb_words))
-        wb_rows = wb_scales[0].bitcast(I32)
         for quad in range(4):
-            nc.sync.dma_start(out=wb_plane[:].bitcast(I32)[32 * quad : 32 * quad + 4], in_=wb_rows[4 * quad : 4 * quad + 4])
+            load_quadrant(nc.sync, wb_scales, wb_plane, quad)
         nc.sync.dma_start(l5[:], offs5)
         nc.sync.dma_start(l6[:], offs6)
 
-        xt_plane = sb.tile([P, T], U8, name="xt_plane")
-        xo_plane = sb.tile([P, Z], U8, name="xo_plane")
         xt_codes = sb.tile([P, J], U16, name="xt_codes", align_bytes=64)
         xt_sc = sb.tile([P, J], U8, name="xt_sc", align_bytes=64)
         xo_codes = sb.tile([P, J], U32, name="xo_codes", align_bytes=64)
         xo_sc = sb.tile([P, J], U8, name="xo_sc", align_bytes=64)
-
-        def spread(plane, stage, base):
-            for h in range(2):
-                nc.vector.tensor_copy(out=plane[:].bitcast(I32)[HALF * h : HALF * (h + 1)], in_=stage[base : base + HALF, h, :])
 
         w_codes = sb.tile([P, PACK, P], U32, name="w_codes", align_bytes=64)
         w0_codes = sb.tile([P, PACK, P], U32, name="w0_codes", align_bytes=64)
@@ -108,16 +114,14 @@ def tile_list_gatedpick_bank_one_pagetwice_kernel(
         wsc = [sb.tile([P, 2, P], U8, name="wsc%d" % t, tag="late%d" % t, align_bytes=64) for t in range(PACK)]
 
         def deal_scales(t):
-            nc.vector.tensor_copy(out=wsc[t][:], in_=ws[:, 0:3:2, :].rearrange("p s (m t) -> p s m t", t=PACK)[:, :, :, t])
+            nc.vector.tensor_copy(out=wsc[t][:], in_=ws[:].rearrange("p s (m t) -> p s m t", t=PACK)[:, :, :, t])
 
-        spread(xt_plane, xt_stage, 0)
+        for quad in range(4):
+            nc.vector.tensor_copy(out=ws32[32 * quad : 32 * quad + 4], in_=ws_stage[:, quad])
         nc.vector.tensor_copy(xt_codes[:], xt_tab[:].indirect(l1[:]))
-        nc.vector.tensor_copy(xt_sc[:], xt_plane[:].indirect(l1[:]))
-        spread(xo_plane, xo_stage, HALF)
-        nc.vector.tensor_copy(xo_codes[:], xo_tab[:].indirect(l2[:]))
-        nc.vector.tensor_copy(out=ws32[HALF:P, 0, :], in_=ws32[0:HALF, 1, :])
-        nc.vector.tensor_copy(out=ws32[0:HALF, 2, :], in_=ws32[HALF:P, 1, :])
         deal_scales(0)
+        nc.vector.tensor_copy(xo_codes[:], xo_tab[:].indirect(l2[:]))
+        nc.vector.tensor_copy(xt_sc[:], xt_plane[:].indirect(l1[:]))
         nc.vector.tensor_copy(xo_sc[:], xo_plane[:].indirect(l2[:]))
 
         picked = sb.tile([P, PACK, O], F32, name="picked")
@@ -167,5 +171,8 @@ def tile_list_gatedpick_bank_one_pagetwice_kernel(
             nc.vector.tensor_copy(page_a[:].indirect(l5[:]), prod[h][:])
             nc.scalar.activation(out=page_b[:].indirect(l6[:]), in_=prod[h][:], func=ACT.Copy)
             total = sb.tile([P, E], F32, name="total%d" % h)
-            nc.vector.tensor_tensor(out=total[:], in0=page_a[:], in1=page_b[:], op=ALU.add)
-            nc.sync.dma_start(out=out[P * h : P * (h + 1), :], in_=total[:])
+            width = E // (h + 1)
+            for first in range(0, E, width):
+                cols = slice(first, first + width)
+                nc.vector.tensor_tensor(out=total[:, cols], in0=page_a[:, cols], in1=page_b[:, cols], op=ALU.add)
+                nc.sync.dma_start(out=out[P * h : P * (h + 1), cols], in_=total[:, cols])

@@ -51,7 +51,7 @@ def tile_list_gatedpick_bank_one_pagetwice_kernel(
         l6 = lists.tile([P, O // 16], U16, name="l6")
 
         xt_plane = sb.tile([P, T], U8, name="xt_plane")
-        xo_plane = sb.tile([P, Z], U8, name="xo_plane")
+        xo_plane = sb.tile([P, Z], U8, name="xo_plane", tag="late2", align_bytes=64)
         ws_stage = sb.tile([4, 4, 2, R // 4], I32, name="ws_stage")
         ws = sb.tile([P, 2, R], U8, name="ws")
         wb_plane = sb.tile([P, N], U8, name="wb_plane", align_bytes=64)
@@ -77,18 +77,17 @@ def tile_list_gatedpick_bank_one_pagetwice_kernel(
         for s, scales in enumerate((w_scales, w0_scales)):
             nc.sync.dma_start(out=ws_stage[:, :, s, :], in_=scales[0].bitcast(I32).rearrange("(q r) c -> r q c", r=4))
         nc.sync.dma_start(l1[:], offs)
+        nc.sync.dma_start(out=xt_tab[:].bitcast(I32), in_=xt_words[0].bitcast(I32))
         nc.sync.dma_start(l2[:], offs2)
         for quad in (0, 1):
             load_quadrant(nc.sync, xt_scales, xt_plane, quad)
-        nc.sync.dma_start(out=xt_tab[:].bitcast(I32), in_=xt_words[0].bitcast(I32))
         nc.sync.dma_start(out=xo_tab[:].bitcast(I32), in_=words_of(xo_words))
+        nc.sync.dma_start(out=w_raw[:].bitcast(I32), in_=words_of(w_words))
         for quad in (2, 3):
             load_quadrant(nc.sync, xt_scales, xt_plane, quad)
-        for quad in (0, 1):
+        for quad in (0, 1, 2):
             load_quadrant(nc.sync, xo_scales, xo_plane, quad)
-        for quad in (2, 3):
-            load_quadrant(nc.gpsimd, xo_scales, xo_plane, quad)
-        nc.sync.dma_start(out=w_raw[:].bitcast(I32), in_=words_of(w_words))
+        load_quadrant(nc.gpsimd, xo_scales, xo_plane, 3)
         nc.sync.dma_start(out=w0_raw[:].bitcast(I32), in_=words_of(w0_words))
         nc.sync.dma_start(l4[:], offs4)
         load_column(sg_t, sg)
@@ -107,34 +106,40 @@ def tile_list_gatedpick_bank_one_pagetwice_kernel(
         xo_sc = sb.tile([P, J], U8, name="xo_sc", align_bytes=64)
 
         w_codes = sb.tile([P, PACK, P], U32, name="w_codes", align_bytes=64)
-        w0_codes = sb.tile([P, PACK, P], U32, name="w0_codes", align_bytes=64)
+        w0_codes = sb.tile([P, PACK, P], U32, name="w0_codes", tag="late3", align_bytes=64)
         for codes, raw in ((w_codes, w_raw), (w0_codes, w0_raw)):
             nc.scalar.copy(out=codes[:].rearrange("p t m -> p m t"), in_=raw[:].rearrange("p (m t) -> p m t", t=PACK))
 
-        wsc = [sb.tile([P, 2, P], U8, name="wsc%d" % t, tag="late%d" % t, align_bytes=64) for t in range(PACK)]
-
-        def deal_scales(t):
-            nc.vector.tensor_copy(out=wsc[t][:], in_=ws[:].rearrange("p s (m t) -> p s m t", t=PACK)[:, :, :, t])
+        ws_by_slot = ws[:].rearrange("p s (m t) -> p t s m", t=PACK)
+        wsc_early = [sb.tile([P, 2, P], U8, name="wsc%d" % t, tag="late%d" % t, align_bytes=64) for t in range(2)]
 
         for quad in range(4):
             nc.vector.tensor_copy(out=ws32[32 * quad : 32 * quad + 4], in_=ws_stage[:, quad])
         nc.vector.tensor_copy(xt_codes[:], xt_tab[:].indirect(l1[:]))
-        deal_scales(0)
+        nc.vector.tensor_copy(out=wsc_early[0][:], in_=ws_by_slot[:, 0])
         nc.vector.tensor_copy(xo_codes[:], xo_tab[:].indirect(l2[:]))
         nc.vector.tensor_copy(xt_sc[:], xt_plane[:].indirect(l1[:]))
         nc.vector.tensor_copy(xo_sc[:], xo_plane[:].indirect(l2[:]))
+
+        nc.vector.tensor_copy(out=wsc_early[1][:], in_=ws_by_slot[:, 1])
+        wsc_late = sb.tile([P, 2, 2, P], U8, name="wsc_late", tag="late2", align_bytes=64)
+        nc.vector.tensor_copy(out=wsc_late[:], in_=ws_by_slot[:, 2:PACK])
+        wsc = [wsc_early[0][:], wsc_early[1][:], wsc_late[:, 0], wsc_late[:, 1]]
 
         picked = sb.tile([P, PACK, O], F32, name="picked")
         gate = sb.tile([P, PACK, O], F32, name="gate")
         hid = sb.tile([P, O, PACK], BF16, name="hid", align_bytes=64)
         for t in range(PACK):
-            if t > 0:
-                deal_scales(t)
             acc = psum.tile([P, J], F32, name="acc%d" % t)
-            nc.tensor.matmul_mx(out=acc[:], lhsT=w_codes[:, t, :].bitcast(E5M2), lhsT_scale=wsc[t][:, 0, :],
-                                rhs=xt_codes[:].bitcast(E2M1), rhs_scale=xt_sc[:], start=True, stop=False)
-            nc.tensor.matmul_mx(out=acc[:], lhsT=w0_codes[:, t, :].bitcast(E4M3), lhsT_scale=wsc[t][:, 1, :],
-                                rhs=xo_codes[:].bitcast(E5M2), rhs_scale=xo_sc[:], start=False, stop=True)
+            passes = [
+                (w_codes[:, t, :].bitcast(E5M2), wsc[t][:, 0, :], xt_codes[:].bitcast(E2M1), xt_sc[:]),
+                (w0_codes[:, t, :].bitcast(E4M3), wsc[t][:, 1, :], xo_codes[:].bitcast(E5M2), xo_sc[:]),
+            ]
+            if t > 1:
+                passes = passes[::-1]
+            for i, (lhs, lhs_sc, rhs, rhs_sc) in enumerate(passes):
+                nc.tensor.matmul_mx(out=acc[:], lhsT=lhs, lhsT_scale=lhs_sc, rhs=rhs, rhs_scale=rhs_sc,
+                                    start=(i == 0), stop=(i == 1))
             a_rows = sb.tile([P, J], F32, name="a%d" % t)
             nc.vector.tensor_copy(out=a_rows[:], in_=acc[:])
             nc.scalar.activation(out=gate[:, t, :], in_=a_rows[:].indirect(l4[:]), func=ACT.Sigmoid,
@@ -167,12 +172,11 @@ def tile_list_gatedpick_bank_one_pagetwice_kernel(
                 nc.scalar.copy(out=rows[:], in_=acc2[:])
             prod.append(rows)
         for h in range(2):
-            page_a, page_b = pages[2 * h], pages[2 * h + 1]
-            nc.vector.tensor_copy(page_a[:].indirect(l5[:]), prod[h][:])
-            nc.scalar.activation(out=page_b[:].indirect(l6[:]), in_=prod[h][:], func=ACT.Copy)
+            nc.vector.tensor_copy(pages[2 * h][:].indirect(l5[:]), prod[h][:])
+            nc.scalar.activation(out=pages[2 * h + 1][:].indirect(l6[:]), in_=prod[h][:], func=ACT.Copy)
+        for h in range(2):
             total = sb.tile([P, E], F32, name="total%d" % h)
-            width = E // (h + 1)
-            for first in range(0, E, width):
-                cols = slice(first, first + width)
-                nc.vector.tensor_tensor(out=total[:, cols], in0=page_a[:, cols], in1=page_b[:, cols], op=ALU.add)
+            for first in range(0, E, E // 2):
+                cols = slice(first, first + E // 2)
+                nc.vector.tensor_tensor(out=total[:, cols], in0=pages[2 * h][:, cols], in1=pages[2 * h + 1][:, cols], op=ALU.add)
                 nc.sync.dma_start(out=out[P * h : P * (h + 1), cols], in_=total[:, cols])

from contextlib import ExitStack

import concourse.mybir as mybir

K, T, J, R, F, Z, O, N, E = 512, 1024, 256, 512, 512, 1024, 128, 256, 512
FLOPS = 2 * K * R * J + 2 * F * R * J + 2 * R * N * O

F32 = mybir.dt.float32
BF16 = mybir.dt.bfloat16
I32 = mybir.dt.int32
U32 = mybir.dt.uint32
U16 = mybir.dt.uint16
U8 = mybir.dt.uint8
E4M3 = mybir.dt.float8_e4m3fn_x4
E5M2 = mybir.dt.float8_e5m2_x4
E2M1 = mybir.dt.float4_e2m1fn_x4
ACT = mybir.ActivationFunctionType
ALU = mybir.AluOpType

P = 128
HALF = 64
PACK = 4


def tile_list_gatedpick_bank_one_pagetwice_kernel(
    tc, xt_words, xt_scales, xo_words, xo_scales, w_words, w_scales, w0_words, w0_scales,
    sa, sg, bg, wb_words, wb_scales, offs, offs2, offs3, offs4, offs5, offs6, out,
):
    nc = tc.nc

    def words_of(packed):
        return packed[0].rearrange("p c b -> p (c b)").bitcast(I32)

    def load_quadrant(engine, scales, plane, quad):
        rows = scales[0].bitcast(I32)
        engine.dma_start(out=plane[:].bitcast(I32)[32 * quad : 32 * quad + 4], in_=rows[4 * quad : 4 * quad + 4])

    def load_column(tile, vec):
        nc.sync.dma_start(out=tile[:], in_=vec.rearrange("(p t) o -> p (t o)", t=PACK))

    with ExitStack() as ctx:
        lists = ctx.enter_context(tc.tile_pool(name="lists", bufs=1))
        sb = ctx.enter_context(tc.tile_pool(name="sb", bufs=1))
        psum = ctx.enter_context(tc.psum_pool(name="psum", bufs=1))

        l1 = lists.tile([P, J // 16], U16, name="l1")
        l2 = lists.tile([P, J // 16], U16, name="l2")
        l3 = lists.tile([P, O // 16], U16, name="l3")
        l4 = lists.tile([P, O // 16], U16, name="l4")
        l5 = lists.tile([P, O // 16], U16, name="l5")
        l6 = lists.tile([P, O // 16], U16, name="l6")

        xt_plane = sb.tile([P, T], U8, name="xt_plane")
        xo_plane = sb.tile([P, Z], U8, name="xo_plane", tag="late2", align_bytes=64)
        ws_stage = sb.tile([4, 4, 2, R // 4], I32, name="ws_stage")
        ws = sb.tile([P, 2, R], U8, name="ws")
        wb_plane = sb.tile([P, N], U8, name="wb_plane", align_bytes=64)
        ws32 = ws[:].bitcast(I32)
        nc.vector.memset(xt_plane[:].bitcast(I32), 0)
        nc.vector.memset(xo_plane[:].bitcast(I32), 0)
        nc.vector.memset(ws32, 0)

        warm_in = sb.tile([P, 1], F32, name="warm_in")
        warm_out = sb.tile([P, 1], F32, name="warm_out")
        nc.vector.memset(warm_in[:], 0.0)
        nc.scalar.activation(out=warm_out[:], in_=warm_in[:], func=ACT.Sigmoid)

        xt_tab = sb.tile([P, T], U16, name="xt_tab")
        xo_tab = sb.tile([P, Z], U32, name="xo_tab")
        w_raw = sb.tile([P, R], U32, name="w_raw")
        w0_raw = sb.tile([P, R], U32, name="w0_raw")
        wb_codes = sb.tile([P, N], U32, name="wb_codes", align_bytes=64)
        sa_t = sb.tile([P, PACK], F32, name="sa_t")
        sg_t = sb.tile([P, PACK], F32, name="sg_t")
        bg_t = sb.tile([P, PACK], F32, name="bg_t")

        for s, scales in enumerate((w_scales, w0_scales)):
            nc.sync.dma_start(out=ws_stage[:, :, s, :], in_=scales[0].bitcast(I32).rearrange("(q r) c -> r q c", r=4))
        nc.sync.dma_start(l1[:], offs)
        nc.sync.dma_start(out=xt_tab[:].bitcast(I32), in_=xt_words[0].bitcast(I32))
        nc.sync.dma_start(l2[:], offs2)
        for quad in (0, 1):
            load_quadrant(nc.sync, xt_scales, xt_plane, quad)
        nc.sync.dma_start(out=xo_tab[:].bitcast(I32), in_=words_of(xo_words))
        nc.sync.dma_start(out=w_raw[:].bitcast(I32), in_=words_of(w_words))
        for quad in (2, 3):
            load_quadrant(nc.sync, xt_scales, xt_plane, quad)
        for quad in (0, 1, 2):
            load_quadrant(nc.sync, xo_scales, xo_plane, quad)
        load_quadrant(nc.gpsimd, xo_scales, xo_plane, 3)
        nc.sync.dma_start(out=w0_raw[:].bitcast(I32), in_=words_of(w0_words))
        nc.sync.dma_start(l4[:], offs4)
        load_column(sg_t, sg)
        load_column(bg_t, bg)
        nc.sync.dma_start(l3[:], offs3)
        load_column(sa_t, sa)
        nc.sync.dma_start(out=wb_codes[:].bitcast(I32), in_=words_of(wb_words))
        for quad in range(4):
            load_quadrant(nc.sync, wb_scales, wb_plane, quad)
        nc.sync.dma_start(l5[:], offs5)
        nc.sync.dma_start(l6[:], offs6)

        xt_codes = sb.tile([P, J], U16, name="xt_codes", align_bytes=64)
        xt_sc = sb.tile([P, J], U8, name="xt_sc", align_bytes=64)
        xo_codes = sb.tile([P, J], U32, name="xo_codes", align_bytes=64)
        xo_sc = sb.tile([P, J], U8, name="xo_sc", align_bytes=64)

        w_codes = sb.tile([P, PACK, P], U32, name="w_codes", align_bytes=64)
        w0_codes = sb.tile([P, PACK, P], U32, name="w0_codes", tag="late3", align_bytes=64)
        for codes, raw in ((w_codes, w_raw), (w0_codes, w0_raw)):
            nc.scalar.copy(out=codes[:].rearrange("p t m -> p m t"), in_=raw[:].rearrange("p (m t) -> p m t", t=PACK))

        ws_by_slot = ws[:].rearrange("p s (m t) -> p t s m", t=PACK)
        wsc_early = [sb.tile([P, 2, P], U8, name="wsc%d" % t, tag="late%d" % t, align_bytes=64) for t in range(2)]

        for quad in range(4):
            nc.vector.tensor_copy(out=ws32[32 * quad : 32 * quad + 4], in_=ws_stage[:, quad])
        nc.vector.tensor_copy(xt_codes[:], xt_tab[:].indirect(l1[:]))
        nc.vector.tensor_copy(out=wsc_early[0][:], in_=ws_by_slot[:, 0])
        nc.vector.tensor_copy(xo_codes[:], xo_tab[:].indirect(l2[:]))
        nc.vector.tensor_copy(xt_sc[:], xt_plane[:].indirect(l1[:]))
        nc.vector.tensor_copy(xo_sc[:], xo_plane[:].indirect(l2[:]))

        nc.vector.tensor_copy(out=wsc_early[1][:], in_=ws_by_slot[:, 1])
        wsc_late = sb.tile([P, 2, 2, P], U8, name="wsc_late", tag="late2", align_bytes=64)
        nc.vector.tensor_copy(out=wsc_late[:], in_=ws_by_slot[:, 2:PACK])
        wsc = [wsc_early[0][:], wsc_early[1][:], wsc_late[:, 0], wsc_late[:, 1]]

        picked = sb.tile([P, PACK, O], F32, name="picked")
        gate = sb.tile([P, PACK, O], F32, name="gate")
        hid = sb.tile([P, O, PACK], BF16, name="hid", align_bytes=64)
        for t in range(PACK):
            acc = psum.tile([P, J], F32, name="acc%d" % t)
            passes = [
                (w_codes[:, t, :].bitcast(E5M2), wsc[t][:, 0, :], xt_codes[:].bitcast(E2M1), xt_sc[:]),
                (w0_codes[:, t, :].bitcast(E4M3), wsc[t][:, 1, :], xo_codes[:].bitcast(E5M2), xo_sc[:]),
            ]
            if t > 1:
                passes = passes[::-1]
            for i, (lhs, lhs_sc, rhs, rhs_sc) in enumerate(passes):
                nc.tensor.matmul_mx(out=acc[:], lhsT=lhs, lhsT_scale=lhs_sc, rhs=rhs, rhs_scale=rhs_sc,
                                    start=(i == 0), stop=(i == 1))
            a_rows = sb.tile([P, J], F32, name="a%d" % t)
            nc.vector.tensor_copy(out=a_rows[:], in_=acc[:])
            nc.scalar.activation(out=gate[:, t, :], in_=a_rows[:].indirect(l4[:]), func=ACT.Sigmoid,
                                 bias=bg_t[:, t : t + 1], scale=sg_t[:, t : t + 1])
            nc.scalar.activation(out=picked[:, t, :], in_=a_rows[:].indirect(l3[:]), func=ACT.Copy,
                                 scale=sa_t[:, t : t + 1])
            if t % 2 == 1:
                pair = slice(t - 1, t + 1)
                nc.vector.tensor_tensor(out=hid[:, :, pair], in0=picked[:, pair, :].rearrange("p t o -> p o t"),
                                        in1=gate[:, pair, :].rearrange("p t o -> p o t"), op=ALU.mult)

        hid_codes = sb.tile([P, O], U32, name="hid_codes", align_bytes=64)
        hid_sc = sb.tile([P, O], U8, name="hid_sc", align_bytes=64)
        nc.vector.quantize_mx(out=hid_codes[:].bitcast(E5M2), scales=hid_sc[:], in_=hid[:].rearrange("p o t -> p (o t)"))

        pages = [sb.tile([P, E], F32, name="page%d" % i, tag="late%d" % i, align_bytes=64) for i in range(4)]
        for page in pages:
            nc.gpsimd.memset(page[:], 0.0)

        prod = []
        for h in range(2):
            cols = slice(P * h, P * (h + 1))
            acc2 = psum.tile([P, O], F32, name="acc2_%d" % h)
            nc.tensor.matmul_mx(out=acc2[:], lhsT=wb_codes[:, cols].bitcast(E4M3), lhsT_scale=wb_plane[:, cols],
                                rhs=hid_codes[:].bitcast(E5M2), rhs_scale=hid_sc[:], start=True, stop=True)
            rows = sb.tile([P, O], F32, name="prod%d" % h)
            if h == 0:
                nc.vector.tensor_copy(out=rows[:], in_=acc2[:])
            else:
                nc.scalar.copy(out=rows[:], in_=acc2[:])
            prod.append(rows)
        for h in range(2):
            nc.vector.tensor_copy(pages[2 * h][:].indirect(l5[:]), prod[h][:])
            nc.scalar.activation(out=pages[2 * h + 1][:].indirect(l6[:]), in_=prod[h][:], func=ACT.Copy)
        for h in range(2):
            total = sb.tile([P, E], F32, name="total%d" % h)
            for first in range(0, E, E // 2):
                cols = slice(first, first + E // 2)
                nc.vector.tensor_tensor(out=total[:, cols], in0=pages[2 * h][:, cols], in1=pages[2 * h + 1][:, cols], op=ALU.add)
                nc.sync.dma_start(out=out[P * h : P * (h + 1), cols], in_=total[:, cols])
